import numpy as np
import ml_dtypes


def mxq(x, axis, fmt="e4m3"):
    dtype, down = {"e4m3": (ml_dtypes.float8_e4m3fn, 7), "e5m2": (ml_dtypes.float8_e5m2, 14)}[fmt]
    v = np.moveaxis(np.asarray(x, np.float32).astype(ml_dtypes.bfloat16).astype(np.float64), axis, -1)
    blocks = v.reshape(v.shape[:-1] + (-1, 32))
    amax = np.abs(blocks).max(-1, keepdims=True)
    byte = np.maximum(np.where(amax > 0, np.frexp(amax)[1] - 1 + 127, 0) - down, 1)
    scale = np.exp2(byte - 127.0)
    codes = (blocks / scale).astype(np.float32).astype(dtype).astype(np.float64)
    return np.moveaxis((codes * scale).reshape(v.shape), -1, axis)


WIDE = False


def mx_kscale(k):
    if not WIDE:
        return np.ones(k)
    levels = np.array([10, -10, 5, -5, 0])
    if k % 512:
        return np.exp2(np.random.permutation(np.resize(levels, k // 32))).repeat(32)
    a = np.empty((k // 512, 16))
    for p in range(k // 512):
        a[p, :8] = np.random.permutation(np.resize(levels, 8))
        for g in range(8):
            far = levels[np.abs(levels - a[p, g]) >= 10]
            a[p, g + 8] = far[np.random.randint(len(far))]
    return np.exp2(a.ravel()).repeat(32)


def f64(x):
    return np.asarray(x).astype(np.float64)


def striped(idx):
    return np.tile(idx.reshape(-1, 16).T, (8, 1)).astype(np.uint16)


def unstriped(offs):
    return offs[:16].T.reshape(-1).astype(np.int64)


def striped8(idx):
    return np.concatenate([x.reshape(-1, 16).T for x in idx]).astype(np.uint16)


def runs(offs, k):
    lists = np.stack([offs[16 * r : 16 * r + 16].T.reshape(-1) for r in range(8)]).astype(np.int64)
    return lists[np.arange(k) % 512 // 64]


def pack_weight(w):
    k, n = w.shape
    w = f64(np.asarray(w, np.float32).astype(ml_dtypes.bfloat16)).reshape(k // 32, 32, n)
    amax = np.abs(w).max(1)
    byte = np.clip(np.where(amax > 0, np.frexp(amax)[1] - 1 + 127 - 7, 1), 1, 254)
    scaled = (w * np.exp2(127.0 - byte)[:, None, :]).reshape(k, n).astype(np.float32)
    words = np.ascontiguousarray(scaled.reshape(k // 512, 128, 4, n).transpose(0, 1, 3, 2)).astype(ml_dtypes.float8_e4m3fn).view(np.uint8)
    return words, np.ascontiguousarray(byte.astype(np.uint8).reshape(k // 512, 16, n))


def unpack_weight(words, scales):
    g, p, n, _ = words.shape
    vals = np.ascontiguousarray(words).view(ml_dtypes.float8_e4m3fn).astype(np.float64) * np.repeat(np.exp2(scales.astype(np.float64) - 127.0), 8, axis=1)[..., None]
    return vals.transpose(0, 1, 3, 2).reshape(g * 512, n)


K, T, S, H, W, G, U = 512, 1024, 256, 512, 128, 2048, 1024


def setup_inputs():
    n = np.random.standard_normal
    s = mx_kscale(K)[:, None]
    packed_xT = pack_weight(n((K, T)) * s)
    packed_dT = pack_weight(n((K, G)) / s)
    return {
        "x_words": packed_xT[0],
        "x_scales": packed_xT[1],
        "w1": (n((K, H)) / np.sqrt(2 * K) / s).astype(np.float32),
        "w2": (n((K, H)) / np.sqrt(2 * K) / s).astype(np.float32),
        "gs": (np.random.uniform(0.5, 1.5, (K, 1)) * s).astype(np.float32),
        "d_words": packed_dT[0],
        "d_scales": packed_dT[1],
        "mem": n((H, U)).astype(np.float32),
        "offs": striped(np.random.permutation(T)[:S]),
        "hz": striped8(np.random.randint(0, T, (8, S))),
        "n1": striped(np.random.permutation(S)[:W]),
        "n2": striped(np.random.permutation(S)[:W]),
        "n3": striped(np.random.permutation(S)),
        "k1": striped8(np.random.randint(0, G, (8, H))),
        "n4": striped(np.random.permutation(U)[:S]),
    }


def reference(x_words, x_scales, w1, w2, gs, d_words, d_scales, mem, offs, hz, n1, n2, n3, k1, n4):
    d_k1 = unpack_weight(d_words, d_scales)[np.arange(K)[:, None], runs(k1, K)]
    xq = unpack_weight(x_words, x_scales)[:, unstriped(offs)]
    x_hz = unpack_weight(x_words, x_scales)[np.arange(K)[:, None], runs(hz, K)]
    y = mxq(f64(w1), 0, "e4m3").T @ xq + mxq(f64(w2), 0, "e4m3").T @ x_hz
    pa = y[:, unstriped(n2)]
    ds = y.copy()
    ds[:, unstriped(n1)] = pa
    z = f64(gs) * (ds - (0.5 * ds[:, unstriped(n3)]))
    h = 0.0625 * ((d_k1.T @ mxq(z, 0, "e4m3")))
    nw = np.maximum(h, 0.5 * f64(mem)[:, unstriped(n4)])
    out = f64(mem).copy()
    out[:, unstriped(n4)] = nw
    return out

@@ -1,0 +1,202 @@
+from contextlib import ExitStack
+
+import concourse.mybir as mybir
+
+K, T, S, H, W, G, U = 512, 1024, 256, 512, 128, 2048, 1024
+FLOPS = 3 * 2 * K * H * S
+
+F32 = mybir.dt.float32
+BF16 = mybir.dt.bfloat16
+I32 = mybir.dt.int32
+U32 = mybir.dt.uint32
+U16 = mybir.dt.uint16
+U8 = mybir.dt.uint8
+FP8X4 = mybir.dt.float8_e4m3fn_x4
+COPY = mybir.ActivationFunctionType.Copy
+MULT = mybir.AluOpType.mult
+MAX = mybir.AluOpType.max
+ADD = mybir.AluOpType.add
+
+P = 128
+PACK = 4
+BLOCKS = H // P
+HALF = S // 2
+ORDER = (3, 0, 1, 2)
+
+
+def load_scale_rows(queue, table, scales):
+    rows = scales[0].bitcast(I32)
+    for b in range(2):
+        queue.dma_start(out=table[b:P:16, :].bitcast(I32), in_=rows[b:16:2, :])
+
+
+def place_scale_rows(nc, queue, plane, picked):
+    nc.vector.tensor_copy(out=plane[:].bitcast(I32), in_=picked[:].bitcast(I32))
+    for b in range(2):
+        queue.dma_start(out=plane[2 + b : P : 32, :].bitcast(I32), in_=picked[16 + b : P : 32, :].bitcast(I32))
+
+
+def tile_picked_thqksetpagex_none_p_kernel(
+    tc, x_words, x_scales, w1, w2, gs, d_words, d_scales, mem, offs, hz, n1, n2, n3, k1, n4, out
+):
+    nc = tc.nc
+    with ExitStack() as ctx:
+        lists = ctx.enter_context(tc.tile_pool(name="lists", bufs=1))
+        sb = ctx.enter_context(tc.tile_pool(name="sb", bufs=1))
+        ps = ctx.enter_context(tc.psum_pool(name="ps", bufs=1))
+
+        def load_list(src, name):
+            tile = lists.tile(list(src.shape), U16, name=name)
+            nc.sync.dma_start(tile[:], src)
+            return tile
+
+        xs_tab = sb.tile([P, T], U8, name="xs_tab")
+        nc.gpsimd.memset(xs_tab[:].bitcast(I32), 0)
+        ds_tab = sb.tile([P, G], U8, name="ds_tab", tag="ds_tab", align_bytes=64)
+        nc.gpsimd.memset(ds_tab[:].bitcast(I32), 0)
+
+        w1_raw = sb.tile([P, PACK, H], F32, name="w1_raw", align_bytes=64)
+        nc.sync.dma_start(out=w1_raw[:], in_=w1.rearrange("(p j) n -> p j n", j=PACK))
+        hz_l = load_list(hz, "hz_l")
+        load_scale_rows(nc.sync, xs_tab, x_scales)
+        offs_l = load_list(offs, "offs_l")
+        xw_tab = sb.tile([P, T], U32, name="xw_tab", align_bytes=64)
+        nc.sync.dma_start(out=xw_tab[:].bitcast(I32), in_=x_words[0].rearrange("p n t -> p (n t)").bitcast(I32))
+        w2_raw = []
+        for piece in range(2):
+            tile = sb.tile([P, PACK, H // 2], F32, name="w2_raw%d" % piece, align_bytes=64)
+            nc.sync.dma_start(out=tile[:], in_=w2.rearrange("(p j) n -> p j n", j=PACK)[:, :, piece * H // 2 : (piece + 1) * H // 2])
+            w2_raw.append(tile)
+        n2_l = load_list(n2, "n2_l")
+        gs_t = sb.tile([P, PACK], F32, name="gs_t", tag="gs_t")
+        nc.sync.dma_start(out=gs_t[:], in_=gs.rearrange("(p t) o -> p (t o)", t=PACK))
+        n1_l = load_list(n1, "n1_l")
+
+        xs_pick = sb.tile([P, 2 * S], U8, name="xs_pick", align_bytes=64)
+        nc.vector.tensor_copy(out=xs_pick[:, S : 2 * S], in_=xs_tab[:].indirect(hz_l[:]))
+        nc.vector.tensor_copy(out=xs_pick[:, 0:S], in_=xs_tab[:].indirect(offs_l[:]))
+        xs_plane = sb.tile([P, 2 * S], U8, name="xs_plane", align_bytes=64)
+        place_scale_rows(nc, nc.sync, xs_plane, xs_pick)
+        x_pick = []
+        for which, lst in enumerate((offs_l, hz_l)):
+            tile = sb.tile([P, S], U32, name="x_pick%d" % which, align_bytes=64)
+            nc.vector.tensor_copy(out=tile[:], in_=xw_tab[:].indirect(lst[:]))
+            x_pick.append(tile)
+
+        dw_tab = sb.tile([P, G], U32, name="dw_tab", tag="dw_tab", align_bytes=64)
+        nc.sync.dma_start(out=dw_tab[:].bitcast(I32), in_=d_words[0].rearrange("p n t -> p (n t)").bitcast(I32))
+        n3_l = load_list(n3, "n3_l")
+        k1_l = load_list(k1, "k1_l")
+        load_scale_rows(nc.sync, ds_tab, d_scales)
+        n4_l = load_list(n4, "n4_l")
+        page = []
+        for c in range(BLOCKS):
+            tile = sb.tile([P, U], F32, name="page%d" % c, align_bytes=64)
+            nc.sync.dma_start(out=tile[:], in_=mem[c * P : (c + 1) * P, :])
+            page.append(tile)
+
+        grouped = [sb.tile([P, PACK, P, PACK], BF16, name="w_grouped%d" % which, align_bytes=64) for which in range(2)]
+        codes = [sb.tile([P, H], U32, name="w_codes%d" % which, align_bytes=64) for which in range(2)]
+        scales = [sb.tile([P, H], U8, name="w_scales%d" % which, align_bytes=64) for which in range(2)]
+
+        def deal(which, raw, m0):
+            src = raw[:].rearrange("p j (m t) -> p m j t", t=PACK)
+            dst = grouped[which][:, :, m0 : m0 + src.shape[1], :].rearrange("p t m j -> p m j t")
+            return dst, src
+
+        dst, src = deal(0, w1_raw, 0)
+        nc.scalar.activation(out=dst, in_=src, func=COPY)
+        nc.vector.quantize_mx(out=codes[0][:].bitcast(FP8X4), scales=scales[0][:], in_=grouped[0][:].rearrange("p t m j -> p (t m j)"))
+        dst, src = deal(1, w2_raw[0], 0)
+        nc.scalar.activation(out=dst, in_=src, func=COPY)
+        dst, src = deal(1, w2_raw[1], P // 2)
+        nc.vector.tensor_copy(out=dst, in_=src)
+        for t in range(PACK):
+            cols = slice(t * P, (t + 1) * P)
+            nc.vector.quantize_mx(out=codes[1][:, cols].bitcast(FP8X4), scales=scales[1][:, cols], in_=grouped[1][:, t].rearrange("p m j -> p (m j)"))
+
+        y_acc = [ps.tile([P, S], F32, name="y_acc%d" % t) for t in range(PACK)]
+        for which in range(2):
+            for t in range(PACK):
+                cols = slice(t * P, (t + 1) * P)
+                nc.tensor.matmul_mx(
+                    out=y_acc[t][:],
+                    lhsT=codes[which][:, cols].bitcast(FP8X4),
+                    lhsT_scale=scales[which][:, cols],
+                    rhs=x_pick[which][:].bitcast(FP8X4),
+                    rhs_scale=xs_plane[:, which * S : (which + 1) * S],
+                    start=(which == 0),
+                    stop=(which == 1),
+                )
+
+        y_rows = [sb.tile([P, S], F32, name="y_rows%d" % t) for t in range(PACK)]
+        ds_rows = [sb.tile([P, S], F32, name="ds_rows%d" % t) for t in range(PACK)]
+        pa = [sb.tile([P, W], F32, name="pa%d" % t) for t in range(PACK)]
+
+        def weigh(rows, t):
+            nc.vector.tensor_scalar(out=rows[t][:], in0=y_acc[t][:], scalar1=gs_t[:, t : t + 1], scalar2=None, op0=MULT)
+
+        for step in range(PACK + 1):
+            if step < PACK:
+                weigh(y_rows, step)
+                nc.scalar.activation(out=pa[step][:], in_=y_rows[step][:].indirect(n2_l[:]), func=COPY)
+            if step > 0:
+                weigh(ds_rows, step - 1)
+                nc.scalar.activation(out=ds_rows[step - 1][:].indirect(n1_l[:]), in_=pa[step - 1][:], func=COPY)
+
+        ds_pick = sb.tile([P, H], U8, name="ds_pick", align_bytes=64)
+        nc.vector.tensor_copy(out=ds_pick[:], in_=ds_tab[:].indirect(k1_l[:]))
+        ds_plane = sb.tile([P, H], U8, name="ds_plane", align_bytes=64)
+        place_scale_rows(nc, nc.sync, ds_plane, ds_pick)
+        d_pick = sb.tile([P, H], U32, name="d_pick", tag="ds_tab", align_bytes=64)
+        nc.vector.tensor_copy(out=d_pick[:], in_=dw_tab[:].indirect(k1_l[:]))
+
+        other = sb.tile([P, 2, PACK, HALF], F32, name="other", tag="gs_t")
+        z_planes = sb.tile([P, 2, PACK, HALF], BF16, name="z_planes", tag="dw_tab", align_bytes=64)
+        h_acc = []
+        for half in range(2):
+            cols = slice(half * HALF, (half + 1) * HALF)
+            lst = n3_l[:, half * HALF // 16 : (half + 1) * HALF // 16]
+            for t in range(PACK):
+                nc.scalar.activation(out=other[:, half, t, :], in_=ds_rows[t][:].indirect(lst), func=COPY, scale=-0.5)
+                nc.vector.tensor_tensor(out=z_planes[:, half, t, :], in0=ds_rows[t][:, cols], in1=other[:, half, t, :], op=ADD)
+            z_grouped = sb.tile([P, HALF, PACK], BF16, name="z_grouped%d" % half, align_bytes=64)
+            nc.vector.tensor_copy(
+                out=z_grouped[:].rearrange("p (a i) t -> p a t i", i=4),
+                in_=z_planes[:, half].rearrange("p t (a i) -> p a t i", i=4),
+            )
+            z_codes = sb.tile([P, HALF], U32, name="z_codes%d" % half, align_bytes=64)
+            z_scales = sb.tile([P, HALF], U8, name="z_scales%d" % half, align_bytes=64)
+            nc.vector.quantize_mx(out=z_codes[:].bitcast(FP8X4), scales=z_scales[:], in_=z_grouped[:].rearrange("p n t -> p (n t)"))
+            acc = ps.tile([P, BLOCKS, HALF], F32, name="h_acc%d" % half)
+            for c in ORDER:
+                nc.tensor.matmul_mx(
+                    out=acc[:, c, :],
+                    lhsT=d_pick[:, c * P : (c + 1) * P].bitcast(FP8X4),
+                    lhsT_scale=ds_plane[:, c * P : (c + 1) * P],
+                    rhs=z_codes[:].bitcast(FP8X4),
+                    rhs_scale=z_scales[:],
+                    start=True,
+                    stop=True,
+                )
+            h_acc.append(acc)
+
+        old = sb.tile([P, BLOCKS, S], F32, name="old")
+        for c in range(BLOCKS):
+            nc.scalar.activation(out=old[:, c, :], in_=page[c][:].indirect(n4_l[:]), func=COPY, scale=0.5)
+
+        new = [sb.tile([P, S], F32, name="new%d" % c) for c in range(BLOCKS)]
+        for c in ORDER:
+            for half in range(2):
+                cols = slice(half * HALF, (half + 1) * HALF)
+                nc.vector.scalar_tensor_tensor(
+                    out=new[c][:, cols], in0=h_acc[half][:, c, :], scalar=0.0625, in1=old[:, c, cols], op0=MULT, op1=MAX
+                )
+
+        for c in ORDER:
+            pieces = 2 if c == ORDER[0] else 1
+            width = S // pieces
+            for i in range(pieces):
+                lst = n4_l[:, i * width // 16 : (i + 1) * width // 16]
+                nc.scalar.activation(out=page[c][:].indirect(lst), in_=new[c][:, i * width : (i + 1) * width], func=COPY)
+            nc.sync.dma_start(out=out[c * P : (c + 1) * P, :], in_=page[c][:])

@@ -21,7 +21,6 @@ P = 128
 PACK = 4
 BLOCKS = H // P
 HALF = S // 2
-ORDER = (3, 0, 1, 2)
 
 
 def load_scale_rows(queue, table, scales):
@@ -77,11 +76,6 @@ def tile_picked_thqksetpagex_none_p_kernel(
         nc.vector.tensor_copy(out=xs_pick[:, 0:S], in_=xs_tab[:].indirect(offs_l[:]))
         xs_plane = sb.tile([P, 2 * S], U8, name="xs_plane", align_bytes=64)
         place_scale_rows(nc, nc.sync, xs_plane, xs_pick)
-        x_pick = []
-        for which, lst in enumerate((offs_l, hz_l)):
-            tile = sb.tile([P, S], U32, name="x_pick%d" % which, align_bytes=64)
-            nc.vector.tensor_copy(out=tile[:], in_=xw_tab[:].indirect(lst[:]))
-            x_pick.append(tile)
 
         dw_tab = sb.tile([P, G], U32, name="dw_tab", tag="dw_tab", align_bytes=64)
         nc.sync.dma_start(out=dw_tab[:].bitcast(I32), in_=d_words[0].rearrange("p n t -> p (n t)").bitcast(I32))
@@ -95,39 +89,56 @@ def tile_picked_thqksetpagex_none_p_kernel(
             nc.sync.dma_start(out=tile[:], in_=mem[c * P : (c + 1) * P, :])
             page.append(tile)
 
-        grouped = [sb.tile([P, PACK, P, PACK], BF16, name="w_grouped%d" % which, align_bytes=64) for which in range(2)]
         codes = [sb.tile([P, H], U32, name="w_codes%d" % which, align_bytes=64) for which in range(2)]
         scales = [sb.tile([P, H], U8, name="w_scales%d" % which, align_bytes=64) for which in range(2)]
 
-        def deal(which, raw, m0):
-            src = raw[:].rearrange("p j (m t) -> p m j t", t=PACK)
-            dst = grouped[which][:, :, m0 : m0 + src.shape[1], :].rearrange("p t m j -> p m j t")
-            return dst, src
+        def quantise(which, t0, values):
+            cols = slice(t0 * P, (t0 + values.shape[1]) * P)
+            nc.vector.quantize_mx(
+                out=codes[which][:, cols].bitcast(FP8X4), scales=scales[which][:, cols], in_=values.rearrange("p t m j -> p (t m j)")
+            )
 
-        dst, src = deal(0, w1_raw, 0)
-        nc.scalar.activation(out=dst, in_=src, func=COPY)
-        nc.vector.quantize_mx(out=codes[0][:].bitcast(FP8X4), scales=scales[0][:], in_=grouped[0][:].rearrange("p t m j -> p (t m j)"))
-        dst, src = deal(1, w2_raw[0], 0)
-        nc.scalar.activation(out=dst, in_=src, func=COPY)
-        dst, src = deal(1, w2_raw[1], P // 2)
-        nc.vector.tensor_copy(out=dst, in_=src)
-        for t in range(PACK):
-            cols = slice(t * P, (t + 1) * P)
-            nc.vector.quantize_mx(out=codes[1][:, cols].bitcast(FP8X4), scales=scales[1][:, cols], in_=grouped[1][:, t].rearrange("p m j -> p (m j)"))
+        w1_grouped = []
+        for pair in range(2):
+            tile = sb.tile([P, 2, P, PACK], BF16, name="w1_pair%d" % pair, tag="w1_pair%d" % pair, align_bytes=64)
+            src = w1_raw[:].rearrange("p j (m t) -> p m j t", t=PACK)[:, :, :, 2 * pair : 2 * pair + 2]
+            nc.scalar.activation(out=tile[:].rearrange("p t m j -> p m j t"), in_=src, func=COPY)
+            w1_grouped.append(tile)
+        quantise(0, 0, w1_grouped[0][:])
+        x_pick = []
+        for which, lst in enumerate((offs_l, hz_l)):
+            tile = sb.tile([P, S], U32, name="x_pick%d" % which, tag="w1_pair0" if which == 0 else "x_pick1", align_bytes=64)
+            nc.vector.tensor_copy(out=tile[:], in_=xw_tab[:].indirect(lst[:]))
+            x_pick.append(tile)
+
+        w2_grouped = sb.tile([P, PACK, P, PACK], BF16, name="w2_grouped", align_bytes=64)
+        for piece in range(2):
+            src = w2_raw[piece][:].rearrange("p j (m t) -> p m j t", t=PACK)
+            dst = w2_grouped[:, :, piece * P // 2 : (piece + 1) * P // 2, :].rearrange("p t m j -> p m j t")
+            if piece == 0:
+                nc.scalar.activation(out=dst, in_=src, func=COPY)
+            else:
+                nc.vector.tensor_copy(out=dst, in_=src)
+        quantise(1, 0, w2_grouped[:, 0:1])
+        quantise(1, 1, w2_grouped[:, 1:2])
+        quantise(0, 2, w1_grouped[1][:])
+        quantise(1, 2, w2_grouped[:, 2:3])
+        quantise(1, 3, w2_grouped[:, 3:4])
 
         y_acc = [ps.tile([P, S], F32, name="y_acc%d" % t) for t in range(PACK)]
-        for which in range(2):
-            for t in range(PACK):
-                cols = slice(t * P, (t + 1) * P)
-                nc.tensor.matmul_mx(
-                    out=y_acc[t][:],
-                    lhsT=codes[which][:, cols].bitcast(FP8X4),
-                    lhsT_scale=scales[which][:, cols],
-                    rhs=x_pick[which][:].bitcast(FP8X4),
-                    rhs_scale=xs_plane[:, which * S : (which + 1) * S],
-                    start=(which == 0),
-                    stop=(which == 1),
-                )
+        for pair in range(2):
+            for which in range(2):
+                for t in (2 * pair, 2 * pair + 1):
+                    cols = slice(t * P, (t + 1) * P)
+                    nc.tensor.matmul_mx(
+                        out=y_acc[t][:],
+                        lhsT=codes[which][:, cols].bitcast(FP8X4),
+                        lhsT_scale=scales[which][:, cols],
+                        rhs=x_pick[which][:].bitcast(FP8X4),
+                        rhs_scale=xs_plane[:, which * S : (which + 1) * S],
+                        start=(which == 0),
+                        stop=(which == 1),
+                    )
 
         y_rows = [sb.tile([P, S], F32, name="y_rows%d" % t) for t in range(PACK)]
         ds_rows = [sb.tile([P, S], F32, name="ds_rows%d" % t) for t in range(PACK)]
@@ -168,10 +179,11 @@ def tile_picked_thqksetpagex_none_p_kernel(
             z_codes = sb.tile([P, HALF], U32, name="z_codes%d" % half, align_bytes=64)
             z_scales = sb.tile([P, HALF], U8, name="z_scales%d" % half, align_bytes=64)
             nc.vector.quantize_mx(out=z_codes[:].bitcast(FP8X4), scales=z_scales[:], in_=z_grouped[:].rearrange("p n t -> p (n t)"))
-            acc = ps.tile([P, BLOCKS, HALF], F32, name="h_acc%d" % half)
-            for c in ORDER:
+            banks = [ps.tile([P, 2, HALF], F32, name="h_acc%d_%d" % (half, i)) for i in range(2)]
+            acc = [banks[c // 2][:, c % 2, :] for c in range(BLOCKS)]
+            for c in range(BLOCKS):
                 nc.tensor.matmul_mx(
-                    out=acc[:, c, :],
+                    out=acc[c],
                     lhsT=d_pick[:, c * P : (c + 1) * P].bitcast(FP8X4),
                     lhsT_scale=ds_plane[:, c * P : (c + 1) * P],
                     rhs=z_codes[:].bitcast(FP8X4),
@@ -186,17 +198,19 @@ def tile_picked_thqksetpagex_none_p_kernel(
             nc.scalar.activation(out=old[:, c, :], in_=page[c][:].indirect(n4_l[:]), func=COPY, scale=0.5)
 
         new = [sb.tile([P, S], F32, name="new%d" % c) for c in range(BLOCKS)]
-        for c in ORDER:
-            for half in range(2):
-                cols = slice(half * HALF, (half + 1) * HALF)
-                nc.vector.scalar_tensor_tensor(
-                    out=new[c][:, cols], in0=h_acc[half][:, c, :], scalar=0.0625, in1=old[:, c, cols], op0=MULT, op1=MAX
-                )
+        steps = [(c, half) for half in range(2) for c in (0, 1)] + [(c, half) for c in (2, 3) for half in range(2)]
+        for c, half in steps:
+            cols = slice(half * HALF, (half + 1) * HALF)
+            nc.vector.scalar_tensor_tensor(
+                out=new[c][:, cols], in0=h_acc[half][c], scalar=0.0625, in1=old[:, c, cols], op0=MULT, op1=MAX
+            )
 
-        for c in ORDER:
-            pieces = 2 if c == ORDER[0] else 1
-            width = S // pieces
-            for i in range(pieces):
-                lst = n4_l[:, i * width // 16 : (i + 1) * width // 16]
-                nc.scalar.activation(out=page[c][:].indirect(lst), in_=new[c][:, i * width : (i + 1) * width], func=COPY)
+        for half in range(2):
+            for c in (0, 1):
+                lst = n4_l[:, half * HALF // 16 : (half + 1) * HALF // 16]
+                nc.scalar.activation(out=page[c][:].indirect(lst), in_=new[c][:, half * HALF : (half + 1) * HALF], func=COPY)
+                if half == 1:
+                    nc.sync.dma_start(out=out[c * P : (c + 1) * P, :], in_=page[c][:])
+        for c in (2, 3):
+            nc.scalar.activation(out=page[c][:].indirect(n4_l[:]), in_=new[c][:], func=COPY)
             nc.sync.dma_start(out=out[c * P : (c + 1) * P, :], in_=page[c][:])

from contextlib import ExitStack

import concourse.mybir as mybir

K, T, S, H, W, G, U = 512, 1024, 256, 512, 128, 2048, 1024
FLOPS = 3 * 2 * K * H * S

F32 = mybir.dt.float32
BF16 = mybir.dt.bfloat16
I32 = mybir.dt.int32
U32 = mybir.dt.uint32
U16 = mybir.dt.uint16
U8 = mybir.dt.uint8
FP8X4 = mybir.dt.float8_e4m3fn_x4
COPY = mybir.ActivationFunctionType.Copy
MULT = mybir.AluOpType.mult
MAX = mybir.AluOpType.max
ADD = mybir.AluOpType.add

P = 128
PACK = 4
BLOCKS = H // P
HALF = S // 2


def load_scale_rows(queue, table, scales):
    rows = scales[0].bitcast(I32)
    for b in range(2):
        queue.dma_start(out=table[b:P:16, :].bitcast(I32), in_=rows[b:16:2, :])


def place_scale_rows(nc, queue, plane, picked):
    nc.vector.tensor_copy(out=plane[:].bitcast(I32), in_=picked[:].bitcast(I32))
    for b in range(2):
        queue.dma_start(out=plane[2 + b : P : 32, :].bitcast(I32), in_=picked[16 + b : P : 32, :].bitcast(I32))


def tile_picked_thqksetpagex_none_p_kernel(
    tc, x_words, x_scales, w1, w2, gs, d_words, d_scales, mem, offs, hz, n1, n2, n3, k1, n4, out
):
    nc = tc.nc
    with ExitStack() as ctx:
        lists = ctx.enter_context(tc.tile_pool(name="lists", bufs=1))
        sb = ctx.enter_context(tc.tile_pool(name="sb", bufs=1))
        ps = ctx.enter_context(tc.psum_pool(name="ps", bufs=1))

        def load_list(src, name):
            tile = lists.tile(list(src.shape), U16, name=name)
            nc.sync.dma_start(tile[:], src)
            return tile

        xs_tab = sb.tile([P, T], U8, name="xs_tab")
        nc.gpsimd.memset(xs_tab[:].bitcast(I32), 0)
        ds_tab = sb.tile([P, G], U8, name="ds_tab", tag="ds_tab", align_bytes=64)
        nc.gpsimd.memset(ds_tab[:].bitcast(I32), 0)

        w1_raw = sb.tile([P, PACK, H], F32, name="w1_raw", align_bytes=64)
        nc.sync.dma_start(out=w1_raw[:], in_=w1.rearrange("(p j) n -> p j n", j=PACK))
        hz_l = load_list(hz, "hz_l")
        load_scale_rows(nc.sync, xs_tab, x_scales)
        offs_l = load_list(offs, "offs_l")
        xw_tab = sb.tile([P, T], U32, name="xw_tab", align_bytes=64)
        nc.sync.dma_start(out=xw_tab[:].bitcast(I32), in_=x_words[0].rearrange("p n t -> p (n t)").bitcast(I32))
        w2_raw = []
        for piece in range(2):
            tile = sb.tile([P, PACK, H // 2], F32, name="w2_raw%d" % piece, align_bytes=64)
            nc.sync.dma_start(out=tile[:], in_=w2.rearrange("(p j) n -> p j n", j=PACK)[:, :, piece * H // 2 : (piece + 1) * H // 2])
            w2_raw.append(tile)
        n2_l = load_list(n2, "n2_l")
        gs_t = sb.tile([P, PACK], F32, name="gs_t", tag="gs_t")
        nc.sync.dma_start(out=gs_t[:], in_=gs.rearrange("(p t) o -> p (t o)", t=PACK))
        n1_l = load_list(n1, "n1_l")

        xs_pick = sb.tile([P, 2 * S], U8, name="xs_pick", align_bytes=64)
        nc.vector.tensor_copy(out=xs_pick[:, S : 2 * S], in_=xs_tab[:].indirect(hz_l[:]))
        nc.vector.tensor_copy(out=xs_pick[:, 0:S], in_=xs_tab[:].indirect(offs_l[:]))
        xs_plane = sb.tile([P, 2 * S], U8, name="xs_plane", align_bytes=64)
        place_scale_rows(nc, nc.sync, xs_plane, xs_pick)

        dw_tab = sb.tile([P, G], U32, name="dw_tab", tag="dw_tab", align_bytes=64)
        nc.sync.dma_start(out=dw_tab[:].bitcast(I32), in_=d_words[0].rearrange("p n t -> p (n t)").bitcast(I32))
        n3_l = load_list(n3, "n3_l")
        k1_l = load_list(k1, "k1_l")
        load_scale_rows(nc.sync, ds_tab, d_scales)
        n4_l = load_list(n4, "n4_l")
        page = []
        for c in range(BLOCKS):
            tile = sb.tile([P, U], F32, name="page%d" % c, align_bytes=64)
            nc.sync.dma_start(out=tile[:], in_=mem[c * P : (c + 1) * P, :])
            page.append(tile)

        codes = [sb.tile([P, H], U32, name="w_codes%d" % which, align_bytes=64) for which in range(2)]
        scales = [sb.tile([P, H], U8, name="w_scales%d" % which, align_bytes=64) for which in range(2)]

        def quantise(which, t0, values):
            cols = slice(t0 * P, (t0 + values.shape[1]) * P)
            nc.vector.quantize_mx(
                out=codes[which][:, cols].bitcast(FP8X4), scales=scales[which][:, cols], in_=values.rearrange("p t m j -> p (t m j)")
            )

        w1_grouped = []
        for pair in range(2):
            tile = sb.tile([P, 2, P, PACK], BF16, name="w1_pair%d" % pair, tag="w1_pair%d" % pair, align_bytes=64)
            src = w1_raw[:].rearrange("p j (m t) -> p m j t", t=PACK)[:, :, :, 2 * pair : 2 * pair + 2]
            nc.scalar.activation(out=tile[:].rearrange("p t m j -> p m j t"), in_=src, func=COPY)
            w1_grouped.append(tile)
        quantise(0, 0, w1_grouped[0][:])
        x_pick = []
        for which, lst in enumerate((offs_l, hz_l)):
            tile = sb.tile([P, S], U32, name="x_pick%d" % which, tag="w1_pair0" if which == 0 else "x_pick1", align_bytes=64)
            nc.vector.tensor_copy(out=tile[:], in_=xw_tab[:].indirect(lst[:]))
            x_pick.append(tile)

        w2_grouped = sb.tile([P, PACK, P, PACK], BF16, name="w2_grouped", align_bytes=64)
        for piece in range(2):
            src = w2_raw[piece][:].rearrange("p j (m t) -> p m j t", t=PACK)
            dst = w2_grouped[:, :, piece * P // 2 : (piece + 1) * P // 2, :].rearrange("p t m j -> p m j t")
            if piece == 0:
                nc.scalar.activation(out=dst, in_=src, func=COPY)
            else:
                nc.vector.tensor_copy(out=dst, in_=src)
        quantise(1, 0, w2_grouped[:, 0:1])
        quantise(1, 1, w2_grouped[:, 1:2])
        quantise(0, 2, w1_grouped[1][:])
        quantise(1, 2, w2_grouped[:, 2:3])
        quantise(1, 3, w2_grouped[:, 3:4])

        y_acc = [ps.tile([P, S], F32, name="y_acc%d" % t) for t in range(PACK)]
        for pair in range(2):
            for which in range(2):
                for t in (2 * pair, 2 * pair + 1):
                    cols = slice(t * P, (t + 1) * P)
                    nc.tensor.matmul_mx(
                        out=y_acc[t][:],
                        lhsT=codes[which][:, cols].bitcast(FP8X4),
                        lhsT_scale=scales[which][:, cols],
                        rhs=x_pick[which][:].bitcast(FP8X4),
                        rhs_scale=xs_plane[:, which * S : (which + 1) * S],
                        start=(which == 0),
                        stop=(which == 1),
                    )

        y_rows = [sb.tile([P, S], F32, name="y_rows%d" % t) for t in range(PACK)]
        ds_rows = [sb.tile([P, S], F32, name="ds_rows%d" % t) for t in range(PACK)]
        pa = [sb.tile([P, W], F32, name="pa%d" % t) for t in range(PACK)]

        def weigh(rows, t):
            nc.vector.tensor_scalar(out=rows[t][:], in0=y_acc[t][:], scalar1=gs_t[:, t : t + 1], scalar2=None, op0=MULT)

        for step in range(PACK + 1):
            if step < PACK:
                weigh(y_rows, step)
                nc.scalar.activation(out=pa[step][:], in_=y_rows[step][:].indirect(n2_l[:]), func=COPY)
            if step > 0:
                weigh(ds_rows, step - 1)
                nc.scalar.activation(out=ds_rows[step - 1][:].indirect(n1_l[:]), in_=pa[step - 1][:], func=COPY)

        ds_pick = sb.tile([P, H], U8, name="ds_pick", align_bytes=64)
        nc.vector.tensor_copy(out=ds_pick[:], in_=ds_tab[:].indirect(k1_l[:]))
        ds_plane = sb.tile([P, H], U8, name="ds_plane", align_bytes=64)
        place_scale_rows(nc, nc.sync, ds_plane, ds_pick)
        d_pick = sb.tile([P, H], U32, name="d_pick", tag="ds_tab", align_bytes=64)
        nc.vector.tensor_copy(out=d_pick[:], in_=dw_tab[:].indirect(k1_l[:]))

        other = sb.tile([P, 2, PACK, HALF], F32, name="other", tag="gs_t")
        z_planes = sb.tile([P, 2, PACK, HALF], BF16, name="z_planes", tag="dw_tab", align_bytes=64)
        h_acc = []
        for half in range(2):
            cols = slice(half * HALF, (half + 1) * HALF)
            lst = n3_l[:, half * HALF // 16 : (half + 1) * HALF // 16]
            for t in range(PACK):
                nc.scalar.activation(out=other[:, half, t, :], in_=ds_rows[t][:].indirect(lst), func=COPY, scale=-0.5)
                nc.vector.tensor_tensor(out=z_planes[:, half, t, :], in0=ds_rows[t][:, cols], in1=other[:, half, t, :], op=ADD)
            z_grouped = sb.tile([P, HALF, PACK], BF16, name="z_grouped%d" % half, align_bytes=64)
            nc.vector.tensor_copy(
                out=z_grouped[:].rearrange("p (a i) t -> p a t i", i=4),
                in_=z_planes[:, half].rearrange("p t (a i) -> p a t i", i=4),
            )
            z_codes = sb.tile([P, HALF], U32, name="z_codes%d" % half, align_bytes=64)
            z_scales = sb.tile([P, HALF], U8, name="z_scales%d" % half, align_bytes=64)
            nc.vector.quantize_mx(out=z_codes[:].bitcast(FP8X4), scales=z_scales[:], in_=z_grouped[:].rearrange("p n t -> p (n t)"))
            banks = [ps.tile([P, 2, HALF], F32, name="h_acc%d_%d" % (half, i)) for i in range(2)]
            acc = [banks[c // 2][:, c % 2, :] for c in range(BLOCKS)]
            for c in range(BLOCKS):
                nc.tensor.matmul_mx(
                    out=acc[c],
                    lhsT=d_pick[:, c * P : (c + 1) * P].bitcast(FP8X4),
                    lhsT_scale=ds_plane[:, c * P : (c + 1) * P],
                    rhs=z_codes[:].bitcast(FP8X4),
                    rhs_scale=z_scales[:],
                    start=True,
                    stop=True,
                )
            h_acc.append(acc)

        old = sb.tile([P, BLOCKS, S], F32, name="old")
        for c in range(BLOCKS):
            nc.scalar.activation(out=old[:, c, :], in_=page[c][:].indirect(n4_l[:]), func=COPY, scale=0.5)

        new = [sb.tile([P, S], F32, name="new%d" % c) for c in range(BLOCKS)]
        steps = [(c, half) for half in range(2) for c in (0, 1)] + [(c, half) for c in (2, 3) for half in range(2)]
        for c, half in steps:
            cols = slice(half * HALF, (half + 1) * HALF)
            nc.vector.scalar_tensor_tensor(
                out=new[c][:, cols], in0=h_acc[half][c], scalar=0.0625, in1=old[:, c, cols], op0=MULT, op1=MAX
            )

        for half in range(2):
            for c in (0, 1):
                lst = n4_l[:, half * HALF // 16 : (half + 1) * HALF // 16]
                nc.scalar.activation(out=page[c][:].indirect(lst), in_=new[c][:, half * HALF : (half + 1) * HALF], func=COPY)
                if half == 1:
                    nc.sync.dma_start(out=out[c * P : (c + 1) * P, :], in_=page[c][:])
        for c in (2, 3):
            nc.scalar.activation(out=page[c][:].indirect(n4_l[:]), in_=new[c][:], func=COPY)
            nc.sync.dma_start(out=out[c * P : (c + 1) * P, :], in_=page[c][:])
